import numpy as np
import ml_dtypes


def mxq(x, axis, fmt="e4m3"):
    dtype, down = {"e4m3": (ml_dtypes.float8_e4m3fn, 7), "e5m2": (ml_dtypes.float8_e5m2, 14)}[fmt]
    v = np.moveaxis(np.asarray(x, np.float32).astype(ml_dtypes.bfloat16).astype(np.float64), axis, -1)
    blocks = v.reshape(v.shape[:-1] + (-1, 32))
    amax = np.abs(blocks).max(-1, keepdims=True)
    byte = np.maximum(np.where(amax > 0, np.frexp(amax)[1] - 1 + 127, 0) - down, 1)
    scale = np.exp2(byte - 127.0)
    codes = (blocks / scale).astype(np.float32).astype(dtype).astype(np.float64)
    return np.moveaxis((codes * scale).reshape(v.shape), -1, axis)


WIDE = False


def mx_kscale(k):
    if not WIDE:
        return np.ones(k)
    levels = np.array([10, -10, 5, -5, 0])
    if k % 512:
        return np.exp2(np.random.permutation(np.resize(levels, k // 32))).repeat(32)
    a = np.empty((k // 512, 16))
    for p in range(k // 512):
        a[p, :8] = np.random.permutation(np.resize(levels, 8))
        for g in range(8):
            far = levels[np.abs(levels - a[p, g]) >= 10]
            a[p, g + 8] = far[np.random.randint(len(far))]
    return np.exp2(a.ravel()).repeat(32)


def f64(x):
    return np.asarray(x).astype(np.float64)


def striped(idx):
    return np.tile(idx.reshape(-1, 16).T, (8, 1)).astype(np.uint16)


def unstriped(offs):
    return offs[:16].T.reshape(-1).astype(np.int64)


def silu(v):
    return v / (1.0 + np.exp(-np.maximum(v, -700.0)))


K, T, E, C, H, N = 512, 768, 6, 128, 1024, 128


def by_expert(wq, xq):
    return np.concatenate([wq[e].T @ xq[:, e * C:(e + 1) * C] for e in range(E)], axis=1)


def setup_inputs():
    n = np.random.standard_normal
    s = mx_kscale(K)[:, None]
    u = mx_kscale(H)
    return {
        "xT": (n((K, T)) * s).astype(np.float32),
        "w1": (n((E, K, H)) / np.sqrt(K) / s[None] * u[None, None, :]).astype(np.float32),
        "w2": (n((E, H, N)) / np.sqrt(H) / u[None, :, None]).astype(np.float32),
        "gate": np.tile(np.random.uniform(0.2, 1.0, E * C), (N, 1)).astype(np.float32),
        "offs": striped(np.random.permutation(T)[:E * C]),
        "dst": striped(np.random.permutation(T)[:E * C]),
    }


def reference(xT, w1, w2, gate, offs, dst):
    idx = unstriped(offs)
    xq = mxq(f64(xT)[:, idx], 0, "e4m3")
    h = silu(by_expert(mxq(f64(w1), 1, "e4m3"), xq))
    y = by_expert(mxq(f64(w2), 1, "e4m3"), mxq(h, 0, "e4m3"))
    out = np.zeros((N, T))
    out[:, unstriped(dst)] = f64(gate) * y
    return out

@@ -1,0 +1,214 @@
+from contextlib import ExitStack
+
+import concourse.mybir as mybir
+
+K, T, E, C, H, N = 512, 768, 6, 128, 1024, 128
+FLOPS = 2 * E * C * (K * H + H * N)
+
+F32 = mybir.dt.float32
+BF16 = mybir.dt.bfloat16
+U32 = mybir.dt.uint32
+U16 = mybir.dt.uint16
+U8 = mybir.dt.uint8
+FP8X4 = mybir.dt.float8_e4m3fn_x4
+SILU = mybir.ActivationFunctionType.Silu
+MULT = mybir.AluOpType.mult
+
+P = 128
+HALF = 512
+HALVES = H // HALF
+X_LOAD = 384
+X_VECTOR = 256
+GATHER = 256
+
+
+def tile_moe_two_mlp_silu_kernel(tc, xT, w1, w2, gate, offs, dst, out):
+    nc = tc.nc
+    with ExitStack() as ctx:
+        lists = ctx.enter_context(tc.tile_pool(name="lists", bufs=1))
+        keep = ctx.enter_context(tc.tile_pool(name="keep", bufs=1))
+        ring = ctx.enter_context(tc.tile_pool(name="ring", bufs=3))
+        psum_h = ctx.enter_context(tc.psum_pool(name="psum_h", bufs=5))
+        psum_y = ctx.enter_context(tc.psum_pool(name="psum_y", bufs=2))
+
+        offs_sb = lists.tile([P, T // 16], U16, name="offs_sb")
+        dst_sb = lists.tile([P, T // 16], U16, name="dst_sb")
+
+        x_raw = keep.tile([P, 4, T], F32, name="x_raw")
+        w1_raw = [keep.tile([P, 4, H], F32, name=f"w1_raw{e}") for e in range(E)]
+        w2_raw = [keep.tile([P, HALVES, 4, N], F32, name=f"w2_raw{e}") for e in range(E)]
+        gate_a = keep.tile([P, 4 * C], F32, name="gate_a")
+        gate_b = keep.tile([P, 2 * C], F32, name="gate_b")
+
+        def load_w1(e):
+            nc.sync.dma_start(w1_raw[e][:], w1[e].rearrange("(p j) c -> p j c", j=4))
+
+        def load_w1_half(e, half):
+            cols = slice(half * HALF, (half + 1) * HALF)
+            nc.sync.dma_start(w1_raw[e][:, :, cols], w1[e].rearrange("(p j) c -> p j c", j=4)[:, :, cols])
+
+        def load_w2(e):
+            nc.sync.dma_start(w2_raw[e][:], w2[e].rearrange("(s p j) n -> p s j n", s=HALVES, j=4))
+
+        x_rows = xT.rearrange("(p j) t -> p j t", j=4)
+        for lo in range(0, T, X_LOAD):
+            nc.sync.dma_start(x_raw[:, :, lo : lo + X_LOAD], x_rows[:, :, lo : lo + X_LOAD])
+        nc.sync.dma_start(offs_sb[:], offs)
+        for e in range(E):
+            if e in (0, E - 1):
+                load_w1_half(e, 0)
+                load_w1_half(e, 1)
+            else:
+                load_w1(e)
+            if e == 0:
+                nc.sync.dma_start(dst_sb[:], dst)
+            load_w2(e)
+            if e == 0:
+                nc.sync.dma_start(gate_a[:], gate[:, : 4 * C])
+        nc.sync.dma_start(gate_b[:], gate[:, 4 * C :])
+
+        x_codes = keep.tile([P, T], U32, name="x_codes", align_bytes=64)
+        x_scales = keep.tile([P, T], U8, name="x_scales", align_bytes=64)
+        slot_codes = keep.tile([P, T], U32, name="slot_codes", align_bytes=64)
+        slot_scales = keep.tile([P, T], U8, name="slot_scales", align_bytes=64)
+        out_sb = keep.tile([P, T], F32, name="out_sb")
+        nc.gpsimd.memset(x_scales[:], 0)
+
+        warm = keep.tile([P, 1], F32, name="warm")
+        nc.vector.memset(warm[:], 0.0)
+        nc.scalar.activation(warm[:], warm[:], SILU)
+
+        def vcopy(dst_ap, src_ap):
+            nc.vector.tensor_copy(dst_ap, src_ap)
+
+        def scopy(dst_ap, src_ap):
+            nc.scalar.copy(dst_ap, src_ap)
+
+        for copy, lo, hi in (
+            (vcopy, 0, X_VECTOR),
+            (scopy, X_VECTOR, X_LOAD),
+            (vcopy, X_LOAD, X_LOAD + X_VECTOR),
+            (scopy, X_LOAD + X_VECTOR, T),
+        ):
+            x_grouped = keep.tile([P, hi - lo, 4], BF16, name=f"x_grouped{lo}", align_bytes=64)
+            copy(
+                x_grouped[:].rearrange("p (c i) j -> p c j i", i=4),
+                x_raw[:, :, lo:hi].rearrange("p j (c i) -> p c j i", i=4),
+            )
+            nc.vector.quantize_mx(
+                out=x_codes[:, lo:hi].bitcast(FP8X4),
+                scales=x_scales[:, lo:hi],
+                in_=x_grouped[:].rearrange("p c j -> p (c j)"),
+            )
+
+        def gather(lo):
+            picked = offs_sb[:, lo // 16 : (lo + GATHER) // 16]
+            nc.vector.tensor_copy(slot_codes[:, lo : lo + GATHER], x_codes[:].indirect(picked))
+            nc.vector.tensor_copy(slot_scales[:, lo : lo + GATHER], x_scales[:].indirect(picked))
+
+        def copy_w1(copy, e, half):
+            cols = slice(half * HALF, (half + 1) * HALF)
+            grouped = ring.tile([P, 4, 128, 4], BF16, name=f"w1_grouped{half}", align_bytes=64, bufs=2)
+            copy(
+                grouped[:].rearrange("p t m j -> p m j t"),
+                w1_raw[e][:, :, cols].rearrange("p j (m t) -> p m j t", t=4),
+            )
+            return grouped
+
+        def quantize_w1(grouped, half):
+            codes = ring.tile([P, HALF], U32, name=f"w1_codes{half}", align_bytes=64, bufs=2)
+            scales = ring.tile([P, HALF], U8, name=f"w1_scales{half}", align_bytes=64, bufs=2)
+            nc.vector.quantize_mx(
+                out=codes[:].bitcast(FP8X4), scales=scales[:], in_=grouped[:].rearrange("p t m j -> p (t m j)")
+            )
+            return codes, scales
+
+        def first_layer(e, codes, scales):
+            slots = slice(e * C, (e + 1) * C)
+            acc = psum_h.tile([P, 4, C], F32, name="acc_h")
+            for t in range(4):
+                cols = slice(128 * t, 128 * (t + 1))
+                nc.tensor.matmul_mx(
+                    out=acc[:, t, :],
+                    lhsT=codes[:, cols].bitcast(FP8X4),
+                    lhsT_scale=scales[:, cols],
+                    rhs=slot_codes[:, slots].bitcast(FP8X4),
+                    rhs_scale=slot_scales[:, slots],
+                    start=True,
+                    stop=True,
+                )
+            return acc
+
+        def apply_silu(acc):
+            h_grouped = ring.tile([P, C, 4], BF16, name="h_grouped", align_bytes=64, bufs=4)
+            nc.scalar.activation(h_grouped[:], acc[:].rearrange("p t n -> p n t"), SILU)
+            return h_grouped
+
+        def quantize_h(h_grouped):
+            codes = ring.tile([P, C], U32, name="h_codes", align_bytes=64, bufs=4)
+            scales = ring.tile([P, C], U8, name="h_scales", align_bytes=64, bufs=4)
+            nc.vector.quantize_mx(
+                out=codes[:].bitcast(FP8X4), scales=scales[:], in_=h_grouped[:].rearrange("p n t -> p (n t)")
+            )
+            return codes, scales
+
+        def copy_w2(copies, e):
+            grouped = ring.tile([P, HALVES, N, 4], BF16, name="w2_grouped", align_bytes=64)
+            for s, copy in enumerate(copies):
+                copy(
+                    grouped[:, s].rearrange("p (c i) j -> p c j i", i=4),
+                    w2_raw[e][:, s].rearrange("p j (c i) -> p c j i", i=4),
+                )
+            return grouped
+
+        def quantize_w2(grouped):
+            codes = ring.tile([P, HALVES, N], U32, name="w2_codes", align_bytes=64)
+            scales = ring.tile([P, HALVES, N], U8, name="w2_scales", align_bytes=64)
+            nc.vector.quantize_mx(
+                out=codes[:].rearrange("p s n -> p (s n)").bitcast(FP8X4),
+                scales=scales[:].rearrange("p s n -> p (s n)"),
+                in_=grouped[:].rearrange("p s n j -> p (s n j)"),
+            )
+            return codes, scales
+
+        def second_layer(e, w2_q, h_q):
+            codes, scales = w2_q
+            acc = psum_y.tile([P, C], F32, name="acc_y")
+            for s in range(HALVES):
+                nc.tensor.matmul_mx(
+                    out=acc[:],
+                    lhsT=codes[:, s, :].bitcast(FP8X4),
+                    lhsT_scale=scales[:, s, :],
+                    rhs=h_q[s][0][:].bitcast(FP8X4),
+                    rhs_scale=h_q[s][1][:],
+                    start=(s == 0),
+                    stop=(s == HALVES - 1),
+                )
+            y = ring.tile([P, C], F32, name="y")
+            nc.scalar.copy(y[:], acc[:])
+            return y
+
+        def scatter(e, y):
+            gates = gate_a[:, e * C : (e + 1) * C] if e < 4 else gate_b[:, (e - 4) * C : (e - 3) * C]
+            places = dst_sb[:, e * C // 16 : (e + 1) * C // 16]
+            nc.vector.tensor_tensor(out_sb[:].indirect(places), y[:], gates, MULT)
+
+        for lo in range(0, T, GATHER):
+            gather(lo)
+        y = None
+        for e in range(E):
+            grouped_a = copy_w1(scopy, e, 0)
+            grouped_b = copy_w1(vcopy, e, 1)
+            acc_b = first_layer(e, *quantize_w1(grouped_b, 1))
+            if e > 0:
+                scatter(e - 1, y)
+            acc_a = first_layer(e, *quantize_w1(grouped_a, 0))
+            grouped_w2 = copy_w2((vcopy, scopy), e)
+            h_b = apply_silu(acc_b)
+            h_a = apply_silu(acc_a)
+            hq_b = quantize_h(h_b)
+            w2_q = quantize_w2(grouped_w2)
+            hq_a = quantize_h(h_a)
+            y = second_layer(e, w2_q, (hq_a, hq_b))
+        scatter(E - 1, y)
+        nc.sync.dma_start(out, out_sb[:])

@@ -19,7 +19,10 @@ HALF = 512
 HALVES = H // HALF
 X_LOAD = 384
 X_VECTOR = 256
-GATHER = 256
+GATHER = 384
+STAGE = 3072
+W2_AT = 2048
+H_AT = 2560
 
 
 def tile_moe_two_mlp_silu_kernel(tc, xT, w1, w2, gate, offs, dst, out):
@@ -84,43 +87,44 @@ def tile_moe_two_mlp_silu_kernel(tc, xT, w1, w2, gate, offs, dst, out):
         def scopy(dst_ap, src_ap):
             nc.scalar.copy(dst_ap, src_ap)
 
+        def vector_stage():
+            return ring.tile([P, STAGE], BF16, name="vector_stage", align_bytes=64, bufs=2)
+
+        def scalar_stage():
+            return ring.tile([P, STAGE], BF16, name="scalar_stage", align_bytes=64, bufs=2)
+
+        def quantize(codes, scales, stage, lo, width):
+            nc.vector.quantize_mx(out=codes.bitcast(FP8X4), scales=scales, in_=stage[:, lo : lo + width])
+
+        x_stage = vector_stage()
         for copy, lo, hi in (
             (vcopy, 0, X_VECTOR),
             (scopy, X_VECTOR, X_LOAD),
             (vcopy, X_LOAD, X_LOAD + X_VECTOR),
             (scopy, X_LOAD + X_VECTOR, T),
         ):
-            x_grouped = keep.tile([P, hi - lo, 4], BF16, name=f"x_grouped{lo}", align_bytes=64)
             copy(
-                x_grouped[:].rearrange("p (c i) j -> p c j i", i=4),
+                x_stage[:, 4 * lo : 4 * hi].rearrange("p (c i j) -> p c j i", i=4, j=4),
                 x_raw[:, :, lo:hi].rearrange("p j (c i) -> p c j i", i=4),
             )
-            nc.vector.quantize_mx(
-                out=x_codes[:, lo:hi].bitcast(FP8X4),
-                scales=x_scales[:, lo:hi],
-                in_=x_grouped[:].rearrange("p c j -> p (c j)"),
-            )
+            quantize(x_codes[:, lo:hi], x_scales[:, lo:hi], x_stage, 4 * lo, 4 * (hi - lo))
 
         def gather(lo):
             picked = offs_sb[:, lo // 16 : (lo + GATHER) // 16]
             nc.vector.tensor_copy(slot_codes[:, lo : lo + GATHER], x_codes[:].indirect(picked))
             nc.vector.tensor_copy(slot_scales[:, lo : lo + GATHER], x_scales[:].indirect(picked))
 
-        def copy_w1(copy, e, half):
+        def copy_w1(copy, stage, e, half):
             cols = slice(half * HALF, (half + 1) * HALF)
-            grouped = ring.tile([P, 4, 128, 4], BF16, name=f"w1_grouped{half}", align_bytes=64, bufs=2)
             copy(
-                grouped[:].rearrange("p t m j -> p m j t"),
+                stage[:, :W2_AT].rearrange("p (t m j) -> p m j t", t=4, j=4),
                 w1_raw[e][:, :, cols].rearrange("p j (m t) -> p m j t", t=4),
             )
-            return grouped
 
-        def quantize_w1(grouped, half):
+        def quantize_w1(stage, half):
             codes = ring.tile([P, HALF], U32, name=f"w1_codes{half}", align_bytes=64, bufs=2)
             scales = ring.tile([P, HALF], U8, name=f"w1_scales{half}", align_bytes=64, bufs=2)
-            nc.vector.quantize_mx(
-                out=codes[:].bitcast(FP8X4), scales=scales[:], in_=grouped[:].rearrange("p t m j -> p (t m j)")
-            )
+            quantize(codes[:], scales[:], stage, 0, W2_AT)
             return codes, scales
 
         def first_layer(e, codes, scales):
@@ -140,75 +144,70 @@ def tile_moe_two_mlp_silu_kernel(tc, xT, w1, w2, gate, offs, dst, out):
             return acc
 
         def apply_silu(acc):
-            h_grouped = ring.tile([P, C, 4], BF16, name="h_grouped", align_bytes=64, bufs=4)
-            nc.scalar.activation(h_grouped[:], acc[:].rearrange("p t n -> p n t"), SILU)
-            return h_grouped
-
-        def quantize_h(h_grouped):
-            codes = ring.tile([P, C], U32, name="h_codes", align_bytes=64, bufs=4)
-            scales = ring.tile([P, C], U8, name="h_scales", align_bytes=64, bufs=4)
-            nc.vector.quantize_mx(
-                out=codes[:].bitcast(FP8X4), scales=scales[:], in_=h_grouped[:].rearrange("p n t -> p (n t)")
+            stage = ring.tile([P, 4 * C], BF16, name="h_stage", align_bytes=64, bufs=4)
+            nc.scalar.activation(
+                stage[:].rearrange("p (n t) -> p n t", t=4), acc[:].rearrange("p t n -> p n t"), SILU
             )
+            return stage
+
+        def quantize_512(stage, lo, name):
+            codes = ring.tile([P, C], U32, name=f"{name}_codes", align_bytes=64, bufs=2)
+            scales = ring.tile([P, C], U8, name=f"{name}_scales", align_bytes=64, bufs=2)
+            quantize(codes[:], scales[:], stage, lo, 4 * C)
             return codes, scales
 
-        def copy_w2(copies, e):
-            grouped = ring.tile([P, HALVES, N, 4], BF16, name="w2_grouped", align_bytes=64)
-            for s, copy in enumerate(copies):
-                copy(
-                    grouped[:, s].rearrange("p (c i) j -> p c j i", i=4),
-                    w2_raw[e][:, s].rearrange("p j (c i) -> p c j i", i=4),
-                )
-            return grouped
-
-        def quantize_w2(grouped):
-            codes = ring.tile([P, HALVES, N], U32, name="w2_codes", align_bytes=64)
-            scales = ring.tile([P, HALVES, N], U8, name="w2_scales", align_bytes=64)
-            nc.vector.quantize_mx(
-                out=codes[:].rearrange("p s n -> p (s n)").bitcast(FP8X4),
-                scales=scales[:].rearrange("p s n -> p (s n)"),
-                in_=grouped[:].rearrange("p s n j -> p (s n j)"),
+        def copy_w2(copy, stage, e, s):
+            copy(
+                stage[:, W2_AT:H_AT].rearrange("p (c i j) -> p c j i", i=4, j=4),
+                w2_raw[e][:, s].rearrange("p j (c i) -> p c j i", i=4),
             )
-            return codes, scales
 
         def second_layer(e, w2_q, h_q):
-            codes, scales = w2_q
             acc = psum_y.tile([P, C], F32, name="acc_y")
             for s in range(HALVES):
                 nc.tensor.matmul_mx(
                     out=acc[:],
-                    lhsT=codes[:, s, :].bitcast(FP8X4),
-                    lhsT_scale=scales[:, s, :],
+                    lhsT=w2_q[s][0][:].bitcast(FP8X4),
+                    lhsT_scale=w2_q[s][1][:],
                     rhs=h_q[s][0][:].bitcast(FP8X4),
                     rhs_scale=h_q[s][1][:],
                     start=(s == 0),
                     stop=(s == HALVES - 1),
                 )
-            y = ring.tile([P, C], F32, name="y")
-            nc.scalar.copy(y[:], acc[:])
+            return acc
+
+        def empty_y(e, acc):
+            y = w1_raw[e + 1 if e + 1 < E else 0][:, 0, :C]
+            nc.scalar.copy(y, acc[:])
             return y
 
         def scatter(e, y):
             gates = gate_a[:, e * C : (e + 1) * C] if e < 4 else gate_b[:, (e - 4) * C : (e - 3) * C]
             places = dst_sb[:, e * C // 16 : (e + 1) * C // 16]
-            nc.vector.tensor_tensor(out_sb[:].indirect(places), y[:], gates, MULT)
+            nc.vector.tensor_tensor(out_sb[:].indirect(places), y, gates, MULT)
 
         for lo in range(0, T, GATHER):
             gather(lo)
-        y = None
+        acc_y = None
         for e in range(E):
-            grouped_a = copy_w1(scopy, e, 0)
-            grouped_b = copy_w1(vcopy, e, 1)
-            acc_b = first_layer(e, *quantize_w1(grouped_b, 1))
+            s_stage = scalar_stage()
+            v_stage = vector_stage()
+            copy_w1(scopy, s_stage, e, 0)
+            copy_w1(vcopy, v_stage, e, 1)
+            if e > 0:
+                y = empty_y(e - 1, acc_y)
+            acc_b = first_layer(e, *quantize_w1(v_stage, 1))
+            copy_w2(vcopy, v_stage, e, 1)
+            copy_w2(scopy, s_stage, e, 0)
+            acc_a = first_layer(e, *quantize_w1(s_stage, 0))
             if e > 0:
                 scatter(e - 1, y)
-            acc_a = first_layer(e, *quantize_w1(grouped_a, 0))
-            grouped_w2 = copy_w2((vcopy, scopy), e)
             h_b = apply_silu(acc_b)
             h_a = apply_silu(acc_a)
-            hq_b = quantize_h(h_b)
-            w2_q = quantize_w2(grouped_w2)
-            hq_a = quantize_h(h_a)
-            y = second_layer(e, w2_q, (hq_a, hq_b))
-        scatter(E - 1, y)
+            w2_b = quantize_512(v_stage, W2_AT, "w2b")
+            hq_b = quantize_512(h_b, 0, "hb")
+            w2_a = quantize_512(s_stage, W2_AT, "w2a")
+            hq_a = quantize_512(h_a, 0, "ha")
+            acc_y = second_layer(e, (w2_a, w2_b), (hq_a, hq_b))
+        scatter(E - 1, empty_y(E - 1, acc_y))
         nc.sync.dma_start(out, out_sb[:])

@@ -15,14 +15,12 @@ SILU = mybir.ActivationFunctionType.Silu
 MULT = mybir.AluOpType.mult
 
 P = 128
+LATE = 2
 HALF = 512
 HALVES = H // HALF
-X_LOAD = 384
-X_VECTOR = 256
+X_VECTOR = 512
 GATHER = 384
-STAGE = 3072
-W2_AT = 2048
-H_AT = 2560
+STAGE = 2048
 
 
 def tile_moe_two_mlp_silu_kernel(tc, xT, w1, w2, gate, offs, dst, out):
@@ -38,7 +36,7 @@ def tile_moe_two_mlp_silu_kernel(tc, xT, w1, w2, gate, offs, dst, out):
         dst_sb = lists.tile([P, T // 16], U16, name="dst_sb")
 
         x_raw = keep.tile([P, 4, T], F32, name="x_raw")
-        w1_raw = [keep.tile([P, 4, H], F32, name=f"w1_raw{e}") for e in range(E)]
+        w1_raw = [keep.tile([P, 4, H], F32, name=f"w1_raw{e}", align_bytes=64) for e in range(E)]
         w2_raw = [keep.tile([P, HALVES, 4, N], F32, name=f"w2_raw{e}") for e in range(E)]
         gate_a = keep.tile([P, 4 * C], F32, name="gate_a")
         gate_b = keep.tile([P, 2 * C], F32, name="gate_b")
@@ -53,21 +51,22 @@ def tile_moe_two_mlp_silu_kernel(tc, xT, w1, w2, gate, offs, dst, out):
         def load_w2(e):
             nc.sync.dma_start(w2_raw[e][:], w2[e].rearrange("(s p j) n -> p s j n", s=HALVES, j=4))
 
-        x_rows = xT.rearrange("(p j) t -> p j t", j=4)
-        for lo in range(0, T, X_LOAD):
-            nc.sync.dma_start(x_raw[:, :, lo : lo + X_LOAD], x_rows[:, :, lo : lo + X_LOAD])
+        nc.sync.dma_start(x_raw[:], xT.rearrange("(p j) t -> p j t", j=4))
         nc.sync.dma_start(offs_sb[:], offs)
         for e in range(E):
-            if e in (0, E - 1):
+            if e == E - 1:
                 load_w1_half(e, 0)
                 load_w1_half(e, 1)
             else:
                 load_w1(e)
             if e == 0:
                 nc.sync.dma_start(dst_sb[:], dst)
-            load_w2(e)
+            if e < E - LATE:
+                load_w2(e)
             if e == 0:
                 nc.sync.dma_start(gate_a[:], gate[:, : 4 * C])
+        for e in range(E - LATE, E):
+            load_w2(e)
         nc.sync.dma_start(gate_b[:], gate[:, 4 * C :])
 
         x_codes = keep.tile([P, T], U32, name="x_codes", align_bytes=64)
@@ -87,22 +86,14 @@ def tile_moe_two_mlp_silu_kernel(tc, xT, w1, w2, gate, offs, dst, out):
         def scopy(dst_ap, src_ap):
             nc.scalar.copy(dst_ap, src_ap)
 
-        def vector_stage():
-            return ring.tile([P, STAGE], BF16, name="vector_stage", align_bytes=64, bufs=2)
-
-        def scalar_stage():
-            return ring.tile([P, STAGE], BF16, name="scalar_stage", align_bytes=64, bufs=2)
+        def new_stage(name, width, bufs=2):
+            return ring.tile([P, width], BF16, name=name, align_bytes=64, bufs=bufs)
 
         def quantize(codes, scales, stage, lo, width):
             nc.vector.quantize_mx(out=codes.bitcast(FP8X4), scales=scales, in_=stage[:, lo : lo + width])
 
-        x_stage = vector_stage()
-        for copy, lo, hi in (
-            (vcopy, 0, X_VECTOR),
-            (scopy, X_VECTOR, X_LOAD),
-            (vcopy, X_LOAD, X_LOAD + X_VECTOR),
-            (scopy, X_LOAD + X_VECTOR, T),
-        ):
+        x_stage = keep.tile([P, 4 * T], BF16, name="x_stage", align_bytes=64)
+        for copy, lo, hi in ((vcopy, 0, X_VECTOR), (scopy, X_VECTOR, T)):
             copy(
                 x_stage[:, 4 * lo : 4 * hi].rearrange("p (c i j) -> p c j i", i=4, j=4),
                 x_raw[:, :, lo:hi].rearrange("p j (c i) -> p c j i", i=4),
@@ -114,17 +105,19 @@ def tile_moe_two_mlp_silu_kernel(tc, xT, w1, w2, gate, offs, dst, out):
             nc.vector.tensor_copy(slot_codes[:, lo : lo + GATHER], x_codes[:].indirect(picked))
             nc.vector.tensor_copy(slot_scales[:, lo : lo + GATHER], x_scales[:].indirect(picked))
 
-        def copy_w1(copy, stage, e, half):
+        def copy_w1(copy, stage, e, half, t0=0, t1=4):
             cols = slice(half * HALF, (half + 1) * HALF)
             copy(
-                stage[:, :W2_AT].rearrange("p (t m j) -> p m j t", t=4, j=4),
-                w1_raw[e][:, :, cols].rearrange("p j (m t) -> p m j t", t=4),
+                stage[:, HALF * t0 : HALF * t1].rearrange("p (t m j) -> p m j t", t=t1 - t0, j=4),
+                w1_raw[e][:, :, cols].rearrange("p j (m t) -> p m j t", t=4)[:, :, :, t0:t1],
             )
 
-        def quantize_w1(stage, half):
+        def quantize_w1(stage, half, parts):
             codes = ring.tile([P, HALF], U32, name=f"w1_codes{half}", align_bytes=64, bufs=2)
             scales = ring.tile([P, HALF], U8, name=f"w1_scales{half}", align_bytes=64, bufs=2)
-            quantize(codes[:], scales[:], stage, 0, W2_AT)
+            step = HALF // parts
+            for lo in range(0, HALF, step):
+                quantize(codes[:, lo : lo + step], scales[:, lo : lo + step], stage, 4 * lo, 4 * step)
             return codes, scales
 
         def first_layer(e, codes, scales):
@@ -143,22 +136,21 @@ def tile_moe_two_mlp_silu_kernel(tc, xT, w1, w2, gate, offs, dst, out):
                 )
             return acc
 
-        def apply_silu(acc):
-            stage = ring.tile([P, 4 * C], BF16, name="h_stage", align_bytes=64, bufs=4)
+        def apply_silu(acc, stage):
             nc.scalar.activation(
-                stage[:].rearrange("p (n t) -> p n t", t=4), acc[:].rearrange("p t n -> p n t"), SILU
+                stage.rearrange("p (n t) -> p n t", t=4), acc[:].rearrange("p t n -> p n t"), SILU
             )
             return stage
 
-        def quantize_512(stage, lo, name):
-            codes = ring.tile([P, C], U32, name=f"{name}_codes", align_bytes=64, bufs=2)
-            scales = ring.tile([P, C], U8, name=f"{name}_scales", align_bytes=64, bufs=2)
-            quantize(codes[:], scales[:], stage, lo, 4 * C)
+        def quantize_all(stage, name, width):
+            codes = ring.tile([P, width // 4], U32, name=f"{name}_codes", align_bytes=64, bufs=2)
+            scales = ring.tile([P, width // 4], U8, name=f"{name}_scales", align_bytes=64, bufs=2)
+            quantize(codes[:], scales[:], stage, 0, width)
             return codes, scales
 
         def copy_w2(copy, stage, e, s):
             copy(
-                stage[:, W2_AT:H_AT].rearrange("p (c i j) -> p c j i", i=4, j=4),
+                stage[:, 4 * N * s : 4 * N * (s + 1)].rearrange("p (c i j) -> p c j i", i=4, j=4),
                 w2_raw[e][:, s].rearrange("p j (c i) -> p c j i", i=4),
             )
 
@@ -167,8 +159,8 @@ def tile_moe_two_mlp_silu_kernel(tc, xT, w1, w2, gate, offs, dst, out):
             for s in range(HALVES):
                 nc.tensor.matmul_mx(
                     out=acc[:],
-                    lhsT=w2_q[s][0][:].bitcast(FP8X4),
-                    lhsT_scale=w2_q[s][1][:],
+                    lhsT=w2_q[0][:, N * s : N * (s + 1)].bitcast(FP8X4),
+                    lhsT_scale=w2_q[1][:, N * s : N * (s + 1)],
                     rhs=h_q[s][0][:].bitcast(FP8X4),
                     rhs_scale=h_q[s][1][:],
                     start=(s == 0),
@@ -177,37 +169,55 @@ def tile_moe_two_mlp_silu_kernel(tc, xT, w1, w2, gate, offs, dst, out):
             return acc
 
         def empty_y(e, acc):
-            y = w1_raw[e + 1 if e + 1 < E else 0][:, 0, :C]
-            nc.scalar.copy(y, acc[:])
+            y = w1_raw[(e + 2) % E][:, 0, :C]
+            gates = gate_a[:, e * C : (e + 1) * C] if e < 4 else gate_b[:, (e - 4) * C : (e - 3) * C]
+            nc.vector.tensor_tensor(y, acc[:], gates, MULT)
             return y
 
         def scatter(e, y):
-            gates = gate_a[:, e * C : (e + 1) * C] if e < 4 else gate_b[:, (e - 4) * C : (e - 3) * C]
             places = dst_sb[:, e * C // 16 : (e + 1) * C // 16]
-            nc.vector.tensor_tensor(out_sb[:].indirect(places), y, gates, MULT)
+            nc.vector.tensor_copy(out_sb[:].indirect(places), y)
 
         for lo in range(0, T, GATHER):
             gather(lo)
-        acc_y = None
+        acc_h = {}
+        w2_stages = {}
+        acc_y = {}
+
+        def second_half(e):
+            own = new_stage("h_stage", 4 * C, bufs=3)
+            lent = w1_raw[(e + 1) % E][:, 0, HALF : HALF + 2 * C].bitcast(BF16)
+            h_b = apply_silu(acc_h[e, 1], own[:])
+            h_a = apply_silu(acc_h[e, 0], lent)
+            w2_q = quantize_all(w2_stages[e], "w2", HALVES * 4 * N)
+            hq_b = quantize_all(h_b, "hb", 4 * C)
+            hq_a = quantize_all(h_a, "ha", 4 * C)
+            acc_y[e] = second_layer(e, w2_q, (hq_a, hq_b))
+
         for e in range(E):
-            s_stage = scalar_stage()
-            v_stage = vector_stage()
-            copy_w1(scopy, s_stage, e, 0)
-            copy_w1(vcopy, v_stage, e, 1)
+            s_stage = new_stage("s_stage", STAGE)
+            v_stage = new_stage("v_stage", STAGE)
+            if e < E - 1:
+                copy_w1(scopy, s_stage, e, 0)
+                copy_w1(vcopy, v_stage, e, 1)
+                parts = 1
+            else:
+                for half, stage in ((0, s_stage), (1, v_stage)):
+                    copy_w1(vcopy, stage, e, half, 0, 2)
+                    copy_w1(scopy, stage, e, half, 2, 4)
+                parts = 2
+            if e > 1:
+                y = empty_y(e - 2, acc_y[e - 2])
+            acc_h[e, 1] = first_layer(e, *quantize_w1(v_stage, 1, parts))
+            w2_stages[e] = new_stage("w2_stage", HALVES * 4 * N)
+            for s in range(HALVES):
+                copy_w2(scopy if e < E - 1 else vcopy, w2_stages[e], e, s)
+            acc_h[e, 0] = first_layer(e, *quantize_w1(s_stage, 0, parts))
             if e > 0:
-                y = empty_y(e - 1, acc_y)
-            acc_b = first_layer(e, *quantize_w1(v_stage, 1))
-            copy_w2(vcopy, v_stage, e, 1)
-            copy_w2(scopy, s_stage, e, 0)
-            acc_a = first_layer(e, *quantize_w1(s_stage, 0))
-            if e > 0:
-                scatter(e - 1, y)
-            h_b = apply_silu(acc_b)
-            h_a = apply_silu(acc_a)
-            w2_b = quantize_512(v_stage, W2_AT, "w2b")
-            hq_b = quantize_512(h_b, 0, "hb")
-            w2_a = quantize_512(s_stage, W2_AT, "w2a")
-            hq_a = quantize_512(h_a, 0, "ha")
-            acc_y = second_layer(e, (w2_a, w2_b), (hq_a, hq_b))
-        scatter(E - 1, empty_y(E - 1, acc_y))
+                second_half(e - 1)
+            if e > 1:
+                scatter(e - 2, y)
+        second_half(E - 1)
+        for e in (E - 2, E - 1):
+            scatter(e, empty_y(e, acc_y[e]))
         nc.sync.dma_start(out, out_sb[:])

from contextlib import ExitStack

import concourse.mybir as mybir

K, T, E, C, H, N = 512, 768, 6, 128, 1024, 128
FLOPS = 2 * E * C * (K * H + H * N)

F32 = mybir.dt.float32
BF16 = mybir.dt.bfloat16
U32 = mybir.dt.uint32
U16 = mybir.dt.uint16
U8 = mybir.dt.uint8
FP8X4 = mybir.dt.float8_e4m3fn_x4
SILU = mybir.ActivationFunctionType.Silu
MULT = mybir.AluOpType.mult

P = 128
LATE = 2
HALF = 512
HALVES = H // HALF
X_VECTOR = 512
GATHER = 384
STAGE = 2048


def tile_moe_two_mlp_silu_kernel(tc, xT, w1, w2, gate, offs, dst, out):
    nc = tc.nc
    with ExitStack() as ctx:
        lists = ctx.enter_context(tc.tile_pool(name="lists", bufs=1))
        keep = ctx.enter_context(tc.tile_pool(name="keep", bufs=1))
        ring = ctx.enter_context(tc.tile_pool(name="ring", bufs=3))
        psum_h = ctx.enter_context(tc.psum_pool(name="psum_h", bufs=5))
        psum_y = ctx.enter_context(tc.psum_pool(name="psum_y", bufs=2))

        offs_sb = lists.tile([P, T // 16], U16, name="offs_sb")
        dst_sb = lists.tile([P, T // 16], U16, name="dst_sb")

        x_raw = keep.tile([P, 4, T], F32, name="x_raw")
        w1_raw = [keep.tile([P, 4, H], F32, name=f"w1_raw{e}", align_bytes=64) for e in range(E)]
        w2_raw = [keep.tile([P, HALVES, 4, N], F32, name=f"w2_raw{e}") for e in range(E)]
        gate_a = keep.tile([P, 4 * C], F32, name="gate_a")
        gate_b = keep.tile([P, 2 * C], F32, name="gate_b")

        def load_w1(e):
            nc.sync.dma_start(w1_raw[e][:], w1[e].rearrange("(p j) c -> p j c", j=4))

        def load_w1_half(e, half):
            cols = slice(half * HALF, (half + 1) * HALF)
            nc.sync.dma_start(w1_raw[e][:, :, cols], w1[e].rearrange("(p j) c -> p j c", j=4)[:, :, cols])

        def load_w2(e):
            nc.sync.dma_start(w2_raw[e][:], w2[e].rearrange("(s p j) n -> p s j n", s=HALVES, j=4))

        nc.sync.dma_start(x_raw[:], xT.rearrange("(p j) t -> p j t", j=4))
        nc.sync.dma_start(offs_sb[:], offs)
        for e in range(E):
            if e == E - 1:
                load_w1_half(e, 0)
                load_w1_half(e, 1)
            else:
                load_w1(e)
            if e == 0:
                nc.sync.dma_start(dst_sb[:], dst)
            if e < E - LATE:
                load_w2(e)
            if e == 0:
                nc.sync.dma_start(gate_a[:], gate[:, : 4 * C])
        for e in range(E - LATE, E):
            load_w2(e)
        nc.sync.dma_start(gate_b[:], gate[:, 4 * C :])

        x_codes = keep.tile([P, T], U32, name="x_codes", align_bytes=64)
        x_scales = keep.tile([P, T], U8, name="x_scales", align_bytes=64)
        slot_codes = keep.tile([P, T], U32, name="slot_codes", align_bytes=64)
        slot_scales = keep.tile([P, T], U8, name="slot_scales", align_bytes=64)
        out_sb = keep.tile([P, T], F32, name="out_sb")
        nc.gpsimd.memset(x_scales[:], 0)

        warm = keep.tile([P, 1], F32, name="warm")
        nc.vector.memset(warm[:], 0.0)
        nc.scalar.activation(warm[:], warm[:], SILU)

        def vcopy(dst_ap, src_ap):
            nc.vector.tensor_copy(dst_ap, src_ap)

        def scopy(dst_ap, src_ap):
            nc.scalar.copy(dst_ap, src_ap)

        def new_stage(name, width, bufs=2):
            return ring.tile([P, width], BF16, name=name, align_bytes=64, bufs=bufs)

        def quantize(codes, scales, stage, lo, width):
            nc.vector.quantize_mx(out=codes.bitcast(FP8X4), scales=scales, in_=stage[:, lo : lo + width])

        x_stage = keep.tile([P, 4 * T], BF16, name="x_stage", align_bytes=64)
        for copy, lo, hi in ((vcopy, 0, X_VECTOR), (scopy, X_VECTOR, T)):
            copy(
                x_stage[:, 4 * lo : 4 * hi].rearrange("p (c i j) -> p c j i", i=4, j=4),
                x_raw[:, :, lo:hi].rearrange("p j (c i) -> p c j i", i=4),
            )
            quantize(x_codes[:, lo:hi], x_scales[:, lo:hi], x_stage, 4 * lo, 4 * (hi - lo))

        def gather(lo):
            picked = offs_sb[:, lo // 16 : (lo + GATHER) // 16]
            nc.vector.tensor_copy(slot_codes[:, lo : lo + GATHER], x_codes[:].indirect(picked))
            nc.vector.tensor_copy(slot_scales[:, lo : lo + GATHER], x_scales[:].indirect(picked))

        def copy_w1(copy, stage, e, half, t0=0, t1=4):
            cols = slice(half * HALF, (half + 1) * HALF)
            copy(
                stage[:, HALF * t0 : HALF * t1].rearrange("p (t m j) -> p m j t", t=t1 - t0, j=4),
                w1_raw[e][:, :, cols].rearrange("p j (m t) -> p m j t", t=4)[:, :, :, t0:t1],
            )

        def quantize_w1(stage, half, parts):
            codes = ring.tile([P, HALF], U32, name=f"w1_codes{half}", align_bytes=64, bufs=2)
            scales = ring.tile([P, HALF], U8, name=f"w1_scales{half}", align_bytes=64, bufs=2)
            step = HALF // parts
            for lo in range(0, HALF, step):
                quantize(codes[:, lo : lo + step], scales[:, lo : lo + step], stage, 4 * lo, 4 * step)
            return codes, scales

        def first_layer(e, codes, scales):
            slots = slice(e * C, (e + 1) * C)
            acc = psum_h.tile([P, 4, C], F32, name="acc_h")
            for t in range(4):
                cols = slice(128 * t, 128 * (t + 1))
                nc.tensor.matmul_mx(
                    out=acc[:, t, :],
                    lhsT=codes[:, cols].bitcast(FP8X4),
                    lhsT_scale=scales[:, cols],
                    rhs=slot_codes[:, slots].bitcast(FP8X4),
                    rhs_scale=slot_scales[:, slots],
                    start=True,
                    stop=True,
                )
            return acc

        def apply_silu(acc, stage):
            nc.scalar.activation(
                stage.rearrange("p (n t) -> p n t", t=4), acc[:].rearrange("p t n -> p n t"), SILU
            )
            return stage

        def quantize_all(stage, name, width):
            codes = ring.tile([P, width // 4], U32, name=f"{name}_codes", align_bytes=64, bufs=2)
            scales = ring.tile([P, width // 4], U8, name=f"{name}_scales", align_bytes=64, bufs=2)
            quantize(codes[:], scales[:], stage, 0, width)
            return codes, scales

        def copy_w2(copy, stage, e, s):
            copy(
                stage[:, 4 * N * s : 4 * N * (s + 1)].rearrange("p (c i j) -> p c j i", i=4, j=4),
                w2_raw[e][:, s].rearrange("p j (c i) -> p c j i", i=4),
            )

        def second_layer(e, w2_q, h_q):
            acc = psum_y.tile([P, C], F32, name="acc_y")
            for s in range(HALVES):
                nc.tensor.matmul_mx(
                    out=acc[:],
                    lhsT=w2_q[0][:, N * s : N * (s + 1)].bitcast(FP8X4),
                    lhsT_scale=w2_q[1][:, N * s : N * (s + 1)],
                    rhs=h_q[s][0][:].bitcast(FP8X4),
                    rhs_scale=h_q[s][1][:],
                    start=(s == 0),
                    stop=(s == HALVES - 1),
                )
            return acc

        def empty_y(e, acc):
            y = w1_raw[(e + 2) % E][:, 0, :C]
            gates = gate_a[:, e * C : (e + 1) * C] if e < 4 else gate_b[:, (e - 4) * C : (e - 3) * C]
            nc.vector.tensor_tensor(y, acc[:], gates, MULT)
            return y

        def scatter(e, y):
            places = dst_sb[:, e * C // 16 : (e + 1) * C // 16]
            nc.vector.tensor_copy(out_sb[:].indirect(places), y)

        for lo in range(0, T, GATHER):
            gather(lo)
        acc_h = {}
        w2_stages = {}
        acc_y = {}

        def second_half(e):
            own = new_stage("h_stage", 4 * C, bufs=3)
            lent = w1_raw[(e + 1) % E][:, 0, HALF : HALF + 2 * C].bitcast(BF16)
            h_b = apply_silu(acc_h[e, 1], own[:])
            h_a = apply_silu(acc_h[e, 0], lent)
            w2_q = quantize_all(w2_stages[e], "w2", HALVES * 4 * N)
            hq_b = quantize_all(h_b, "hb", 4 * C)
            hq_a = quantize_all(h_a, "ha", 4 * C)
            acc_y[e] = second_layer(e, w2_q, (hq_a, hq_b))

        for e in range(E):
            s_stage = new_stage("s_stage", STAGE)
            v_stage = new_stage("v_stage", STAGE)
            if e < E - 1:
                copy_w1(scopy, s_stage, e, 0)
                copy_w1(vcopy, v_stage, e, 1)
                parts = 1
            else:
                for half, stage in ((0, s_stage), (1, v_stage)):
                    copy_w1(vcopy, stage, e, half, 0, 2)
                    copy_w1(scopy, stage, e, half, 2, 4)
                parts = 2
            if e > 1:
                y = empty_y(e - 2, acc_y[e - 2])
            acc_h[e, 1] = first_layer(e, *quantize_w1(v_stage, 1, parts))
            w2_stages[e] = new_stage("w2_stage", HALVES * 4 * N)
            for s in range(HALVES):
                copy_w2(scopy if e < E - 1 else vcopy, w2_stages[e], e, s)
            acc_h[e, 0] = first_layer(e, *quantize_w1(s_stage, 0, parts))
            if e > 0:
                second_half(e - 1)
            if e > 1:
                scatter(e - 2, y)
        second_half(E - 1)
        for e in (E - 2, E - 1):
            scatter(e, empty_y(e, acc_y[e]))
        nc.sync.dma_start(out, out_sb[:])
